import numpy as np
import ml_dtypes


def mxq(x, axis, fmt="e4m3"):
    dtype, down = {"e4m3": (ml_dtypes.float8_e4m3fn, 7), "e5m2": (ml_dtypes.float8_e5m2, 14)}[fmt]
    v = np.moveaxis(np.asarray(x, np.float32).astype(ml_dtypes.bfloat16).astype(np.float64), axis, -1)
    blocks = v.reshape(v.shape[:-1] + (-1, 32))
    amax = np.abs(blocks).max(-1, keepdims=True)
    byte = np.maximum(np.where(amax > 0, np.frexp(amax)[1] - 1 + 127, 0) - down, 1)
    scale = np.exp2(byte - 127.0)
    codes = (blocks / scale).astype(np.float32).astype(dtype).astype(np.float64)
    return np.moveaxis((codes * scale).reshape(v.shape), -1, axis)


WIDE = False


def mx_kscale(k):
    if not WIDE:
        return np.ones(k)
    levels = np.array([10, -10, 5, -5, 0])
    if k % 512:
        return np.exp2(np.random.permutation(np.resize(levels, k // 32))).repeat(32)
    a = np.empty((k // 512, 16))
    for p in range(k // 512):
        a[p, :8] = np.random.permutation(np.resize(levels, 8))
        for g in range(8):
            far = levels[np.abs(levels - a[p, g]) >= 10]
            a[p, g + 8] = far[np.random.randint(len(far))]
    return np.exp2(a.ravel()).repeat(32)


def f64(x):
    return np.asarray(x).astype(np.float64)


def striped(idx):
    return np.tile(idx.reshape(-1, 16).T, (8, 1)).astype(np.uint16)


def unstriped(offs):
    return offs[:16].T.reshape(-1).astype(np.int64)


E2M1 = np.array([0.0, 0.5, 1.0, 1.5, 2.0, 3.0, 4.0, 6.0, -0.0, -0.5, -1.0, -1.5, -2.0, -3.0, -4.0, -6.0])


def pack_weight(w, fmt):
    k, n = w.shape
    w = f64(np.asarray(w, np.float32).astype(ml_dtypes.bfloat16)).reshape(k // 32, 32, n)
    amax = np.abs(w).max(1)
    if fmt == "e4m3":
        byte = np.frexp(amax)[1] - 1 + 127 - 7
    else:
        mant, ex = np.frexp(amax / 6.0)
        byte = np.where(mant > 0.5, ex, ex - 1) + 127
    byte = np.clip(np.where(amax > 0, byte, 1), 1, 254)
    scaled = (w * np.exp2(127.0 - byte)[:, None, :]).reshape(k, n).astype(np.float32)
    by_word = np.ascontiguousarray(scaled.reshape(k // 512, 128, 4, n).transpose(0, 1, 3, 2))
    if fmt == "e4m3":
        words = by_word.astype(ml_dtypes.float8_e4m3fn).view(np.uint8)
    else:
        c = by_word.astype(ml_dtypes.float4_e2m1fn).view(np.uint8) & 0xF
        words = (c[..., 0::2] | (c[..., 1::2] << 4)).reshape(k // 512, 128, 2 * n)
    return np.ascontiguousarray(words), np.ascontiguousarray(byte.astype(np.uint8).reshape(k // 512, 16, n))


def unpack_weight(words, scales, fmt):
    g, _, n = scales.shape
    words = np.ascontiguousarray(words).reshape(g, 128, n, -1)
    if fmt == "e4m3":
        vals = words.view(ml_dtypes.float8_e4m3fn).astype(np.float64)
    else:
        nib = np.empty((g, 128, n, 4), np.uint8)
        nib[..., 0::2] = words & 0xF
        nib[..., 1::2] = words >> 4
        vals = E2M1[nib]
    vals = vals * np.repeat(np.exp2(scales.astype(np.float64) - 127.0), 8, axis=1)[..., None]
    return vals.transpose(0, 1, 3, 2).reshape(g * 512, n)


def gelu(v):
    return 0.5 * v * (1.0 + np.tanh(np.sqrt(2.0 / np.pi) * (v + 0.044715 * v**3)))


K, T, S, H, T2, P = 1536, 2048, 512, 1024, 1024, 512

def setup_inputs():
    n = np.random.standard_normal
    s = mx_kscale(K)[:, None]
    u = mx_kscale(H)[:, None]
    d = {}
    d["tab_words"], d["tab_scales"] = pack_weight(n((K, T)) * s, "e4m3")
    d["offs"] = striped(np.random.permutation(T)[:S])
    d["offs2"] = striped(np.random.permutation(T2)[:S])
    d["offs3"] = striped(np.random.permutation(T2)[:P])
    d["offs4"] = striped(np.random.permutation(T2)[:P])
    d["w1"] = (n((K, H)) / s / K ** 0.5).astype(np.float32)
    d["gain"] = (np.exp(0.4 * n(H)) * u[:, 0]).astype(np.float32)
    d["wgs"] = np.exp(0.3 * n((128, S))).astype(np.float32)
    d["page0"] = (n((H, T2)) * u).astype(np.float32)
    d["fresh"] = np.exp(0.3 * n(H)).astype(np.float32)
    d["w4_words"], d["w4_scales"] = pack_weight(n((H, H)) / u * u.T / H ** 0.5, "e2m1")
    d["w3"] = (n((H, H)) / u / H ** 0.5).astype(np.float32)
    d["near"] = (np.exp(0.3 * n(H)) / u[:, 0]).astype(np.float32)
    return d

def reference(tab_words, tab_scales, offs, offs2, offs3, offs4, w1, gain, wgs, page0, fresh, w4_words, w4_scales, w3, near):
    v = unpack_weight(tab_words, tab_scales, "e4m3")[:, unstriped(offs)]
    h = f64(gain)[:, None] * (mxq(f64(w1), 0, "e4m3").T @ v)
    page = f64(page0).copy()
    page[:, unstriped(offs2)] = np.tile(f64(wgs), (H // 128, 1)) * h
    x = page[:, unstriped(offs3)] * f64(fresh)[:, None]
    w4 = unpack_weight(w4_words, w4_scales, "e2m1")
    y = w4.T @ mxq(x, 0, "e4m3")
    low = np.minimum(y, x)
    q = mxq(f64(w3), 0, "e4m3").T @ mxq(low, 0, "e4m3")
    nb = np.abs(page[:, unstriped(offs4)] * f64(near)[:, None])
    return q * nb

@@ -1,0 +1,359 @@
+from contextlib import ExitStack
+
+import concourse.mybir as mybir
+
+K, T, S, H, T2, NJ = 1536, 2048, 512, 1024, 1024, 512
+FLOPS = 2 * K * H * S + 2 * 2 * H * H * NJ
+
+F32 = mybir.dt.float32
+BF16 = mybir.dt.bfloat16
+I32 = mybir.dt.int32
+U32 = mybir.dt.uint32
+U16 = mybir.dt.uint16
+U8 = mybir.dt.uint8
+FP8X4 = mybir.dt.float8_e4m3fn_x4
+FP4X4 = mybir.dt.float4_e2m1fn_x4
+MULT = mybir.AluOpType.mult
+MIN = mybir.AluOpType.min
+COPY = mybir.ActivationFunctionType.Copy
+ABS = mybir.ActivationFunctionType.Abs
+
+P = 128
+PACK = 4
+PASS = P * PACK
+HALF = NJ // 2
+QUART = NJ // 4
+
+
+def tile_list_sushi_belt_scores_kernel(
+    tc, tab_words, tab_scales, offs, offs2, offs3, offs4, w1, gain, wgs, page0, fresh,
+    w4_words, w4_scales, w3, near, out,
+):
+    nc = tc.nc
+    with ExitStack() as ctx:
+        keep = ctx.enter_context(tc.tile_pool(name="keep", bufs=1))
+        ring = ctx.enter_context(tc.tile_pool(name="ring", bufs=4))
+        psum = ctx.enter_context(tc.psum_pool(name="psum", bufs=1))
+
+        def kept(shape, dtype, name, tag=None):
+            return keep.tile(shape, dtype, name=name, tag=tag or name, align_bytes=64)
+
+        def bank(index, shape, name):
+            return psum.tile(shape, F32, name=name, tag="bank%d" % index)
+
+        def load_list(src, name):
+            tile = keep.tile([P, 32], U16, name=name)
+            nc.sync.dma_start(tile[:], src)
+            return tile
+
+        def load_rows(src, name):
+            tile = kept([P, 2, PACK], F32, name)
+            nc.sync.dma_start(tile[:], src.rearrange("(b p t) -> p b t", b=2, t=PACK))
+            return tile
+
+        def load_weight(w, a, b):
+            raw = ring.tile([P, PACK, PASS], F32, name="raw", align_bytes=64)
+            nc.sync.dma_start(
+                raw[:], w[a * PASS:(a + 1) * PASS, b * PASS:(b + 1) * PASS].rearrange("(p i) c -> p i c", i=PACK))
+            return raw
+
+        def weave_weight(raw):
+            woven = ring.tile([P, PACK, P, PACK], BF16, name="woven", align_bytes=64)
+            nc.scalar.copy(out=woven[:].rearrange("p t m i -> p m i t"),
+                           in_=raw[:].rearrange("p i (m t) -> p m i t", t=PACK))
+            return woven
+
+        def quantise(woven_flat, codes, scales):
+            nc.vector.quantize_mx(out=codes.bitcast(FP8X4), scales=scales, in_=woven_flat)
+
+        def quantise_weight(woven, codes, name):
+            scales = kept([P, PASS], U8, name + "_scales")
+            quantise(woven[:].rearrange("p t m i -> p (t m i)"), codes, scales[:])
+            return codes, scales
+
+        def load_table(a):
+            tile = kept([P, T], I32, "tab%d" % a)
+            nc.sync.dma_start(tile[:], tab_words[a].rearrange("p t i -> p (t i)").bitcast(I32))
+            return tile
+
+        def load_page(b, t):
+            tile = kept([P, T2], F32, "page%d%d" % (b, t))
+            nc.sync.dma_start(tile[:], page0.rearrange("(b p t) c -> b t p c", b=2, t=PACK)[b][t])
+            return tile
+
+        tab_sc = kept([P, T], U8, "tab_sc")
+        nc.vector.memset(tab_sc[:].bitcast(I32), 0)
+        for q in range(4):
+            nc.scalar.dma_start(tab_sc[32 * q:32 * q + 12, :].bitcast(I32),
+                                tab_scales[:, 4 * q:4 * q + 4, :].bitcast(I32))
+        w4_sc_raw = kept([P, 2 * H], U8, "w4_sc_raw")
+        nc.vector.memset(w4_sc_raw[:].bitcast(I32), 0)
+        for q in range(4):
+            nc.scalar.dma_start(w4_sc_raw[32 * q:32 * q + 4, :].bitcast(I32).rearrange("r (a c) -> r a c", a=2),
+                                w4_scales[:, 4 * q:4 * q + 4, :].rearrange("a r c -> r a c").bitcast(I32))
+
+        w4_raw = kept([P, 4 * H], U8, "w4_raw")
+        nc.sync.dma_start(w4_raw[:].bitcast(I32).rearrange("p (a c) -> p a c", a=2),
+                          w4_words.rearrange("a p c -> p a c").bitcast(I32))
+        raw1 = {}
+        raw1[0, 0] = load_weight(w1, 0, 0)
+        idx = load_list(offs, "idx")
+        raw1[1, 0] = load_weight(w1, 1, 0)
+        tab = [load_table(0)]
+        raw1[2, 0] = load_weight(w1, 2, 0)
+        tab.append(load_table(1))
+        tab.append(load_table(2))
+        gain_sb = load_rows(gain, "gain_sb")
+        idx2 = load_list(offs2, "idx2")
+        page = {}
+        page[0, 0] = load_page(0, 0)
+        wgs_rows = wgs.rearrange("(q t) j -> q t j", t=PACK)
+        wgs_first = kept([P, S], F32, "wgs_first")
+        for g in range(4):
+            nc.sync.dma_start(wgs_first[32 * g:32 * g + 32, :], wgs_rows[:, 0, :])
+        page[0, 1] = load_page(0, 1)
+        wgs_rest = kept([P, PACK - 1, S], F32, "wgs_rest", tag="wgs_then_w3")
+        for g in range(4):
+            nc.sync.dma_start(wgs_rest[32 * g:32 * g + 32, :, :], wgs_rows[:, 1:PACK, :])
+        raw1[0, 1] = load_weight(w1, 0, 1)
+        page[0, 2] = load_page(0, 2)
+
+        w4_codes = kept([P, 4 * H], U8, "w4_codes")
+        w4_sc = kept([P, 2 * H], U8, "w4_sc")
+        for a in range(2):
+            nc.vector.tensor_copy(
+                out=w4_codes[:, a * 2 * H:(a + 1) * 2 * H].bitcast(U16).rearrange("p (b t m) -> p b t m", b=2, t=PACK),
+                in_=w4_raw[:, a * 2 * H:(a + 1) * 2 * H].bitcast(U16).rearrange("p (b m t) -> p b t m", b=2, t=PACK))
+        for a in range(2):
+            nc.vector.tensor_copy(
+                out=w4_sc[:, a * H:(a + 1) * H].rearrange("p (b t m) -> p b t m", b=2, t=PACK),
+                in_=w4_sc_raw[:, a * H:(a + 1) * H].rearrange("p (b m t) -> p b t m", b=2, t=PACK))
+
+        v_sc = kept([P, S], U8, "v_sc")
+        nc.vector.tensor_copy(out=v_sc[:], in_=tab_sc[:].indirect(idx[:]))
+        v = []
+        w1_q = {}
+
+        def prepare_w1(a, b):
+            codes = kept([P, PASS], U32, "w1_codes%d%d" % (a, b))
+            w1_q[a, b] = quantise_weight(weave_weight(raw1[a, b]), codes[:], "w1_%d%d" % (a, b))
+
+        def first_pass(a, b, banks):
+            codes, scales = w1_q[a, b]
+            for t in range(PACK):
+                nc.tensor.matmul_mx(
+                    out=banks[t][:], lhsT=codes[:, t * P:(t + 1) * P].bitcast(FP8X4),
+                    lhsT_scale=scales[:, t * P:(t + 1) * P], rhs=v[a][:].bitcast(FP8X4),
+                    rhs_scale=v_sc[4 * a:P, :], start=(a == 0), stop=(a == 2))
+
+        h = {}
+
+        def leave_h(b, banks):
+            for t in range(PACK):
+                h[b, t] = kept([P, S], F32, "h%d%d" % (b, t))
+                nc.scalar.activation(out=h[b, t][:], in_=banks[t][:], func=COPY, scale=gain_sb[:, b, t:t + 1])
+
+        banks = [bank(t, [P, S], "h_bank0%d" % t) for t in range(PACK)]
+        for a in range(3):
+            prepare_w1(a, 0)
+            v.append(kept([P, S], U32, "v%d" % a))
+            nc.vector.tensor_copy(out=v[a][:], in_=tab[a][:].bitcast(U32).indirect(idx[:]))
+            first_pass(a, 0, banks)
+        leave_h(0, banks)
+
+        reread = {}
+
+        def put(b, t):
+            weights = wgs_first[:] if t == 0 else wgs_rest[:, t - 1, :]
+            nc.vector.tensor_tensor(page[b, t][:].indirect(idx2[:]), h[b, t][:], weights, MULT)
+
+        def fetch(b, t, into):
+            reread[b, t] = into
+            nc.vector.tensor_copy(out=into, in_=page[b, t][:].indirect(idx3[:]))
+
+        def fresh_buffer():
+            tile = ring.tile([P, NJ], F32, name="reread", align_bytes=64)
+            return tile[:]
+
+        x = {(b, half): kept([P, PACK, HALF], F32, "x%d%d" % (b, half)) for b in range(2) for half in range(2)}
+
+        def scale_x(b, t, halves):
+            for half in halves:
+                nc.scalar.activation(out=x[b, half][:, t, :], in_=reread[b, t][:, half * HALF:(half + 1) * HALF],
+                                     func=COPY, scale=fresh_sb[:, b, t:t + 1])
+
+        def weave_x(b, half, woven):
+            nc.scalar.copy(out=woven.rearrange("p (c i) t -> p c t i", i=4),
+                           in_=x[b, half][:].rearrange("p t (c i) -> p c t i", i=4))
+
+        x_q = {}
+
+        def quantise_x(woven_flat, width, name):
+            codes = kept([P, width], U32, name + "_codes")
+            scales = kept([P, width], U8, name + "_scales")
+            quantise(woven_flat, codes[:], scales[:])
+            return codes, scales
+
+        banks = [bank(PACK + t, [P, S], "h_bank1%d" % t) for t in range(PACK)]
+        raw1[1, 1] = load_weight(w1, 1, 1)
+        page[0, 3] = load_page(0, 3)
+        for t in range(3):
+            put(0, t)
+        prepare_w1(0, 1)
+        first_pass(0, 1, banks)
+        raw1[2, 1] = load_weight(w1, 2, 1)
+        put(0, 3)
+        prepare_w1(1, 1)
+        first_pass(1, 1, banks)
+        raw3 = {}
+        raw3[0, 0] = load_weight(w3, 0, 0)
+        page[1, 0] = load_page(1, 0)
+        idx3 = load_list(offs3, "idx3")
+        fresh_sb = load_rows(fresh, "fresh_sb")
+        for t in range(1, PACK):
+            page[1, t] = load_page(1, t)
+        prepare_w1(2, 1)
+        first_pass(2, 1, banks)
+        raw3[1, 0] = load_weight(w3, 1, 0)
+        woven3 = {}
+        leave_h(1, banks)
+        woven3[0, 0] = weave_weight(raw3[0, 0])
+        raw3[0, 1] = load_weight(w3, 0, 1)
+        for t in range(PACK):
+            fetch(0, t, fresh_buffer())
+        for t in range(PACK):
+            scale_x(0, t, (0, 1))
+        x0_woven = kept([P, 2, HALF, PACK], BF16, "x0_woven", tag="x0_woven_then_reread")
+        for half in range(2):
+            weave_x(0, half, x0_woven[:, half, :, :])
+        woven3[1, 0] = weave_weight(raw3[1, 0])
+        raw3[1, 1] = load_weight(w3, 1, 1)
+        idx4 = load_list(offs4, "idx4")
+        near_sb = load_rows(near, "near_sb")
+        woven3[0, 1] = weave_weight(raw3[0, 1])
+        woven3[1, 1] = weave_weight(raw3[1, 1])
+        for t in range(PACK):
+            put(1, t)
+        for t in range(2):
+            fetch(1, t, fresh_buffer())
+        codes, scales = quantise_x(x0_woven[:].rearrange("p h j t -> p (h j t)"), NJ, "x0")
+        for half in range(2):
+            x_q[0, half] = codes[:, half * HALF:(half + 1) * HALF], scales[:, half * HALF:(half + 1) * HALF]
+
+        y_bank = {(half, jj, b): bank(4 * half + 2 * jj + b, [P, PACK, QUART], "y_bank%d%d%d" % (half, jj, b))
+                  for half in range(2) for jj in range(2) for b in range(2)}
+
+        def second_pass(a, half):
+            codes, scales = x_q[a, half]
+            for jj in range(2):
+                for b in range(2):
+                    for t in range(PACK):
+                        col = a * H + b * PASS + t * P
+                        nc.tensor.matmul_mx(
+                            out=y_bank[half, jj, b][:, t, :],
+                            lhsT=w4_codes[:, 2 * col:2 * (col + P)].bitcast(FP4X4),
+                            lhsT_scale=w4_sc[:, col:col + P],
+                            rhs=codes[:, jj * QUART:(jj + 1) * QUART].bitcast(FP8X4),
+                            rhs_scale=scales[:, jj * QUART:(jj + 1) * QUART],
+                            start=(a == 0 and t == 0), stop=(a == 1 and t == PACK - 1))
+
+        for half in range(2):
+            second_pass(0, half)
+        reread_late = kept([P, 2, NJ], F32, "reread_late", tag="x0_woven_then_reread")
+        for t in range(2, PACK):
+            fetch(1, t, reread_late[:, t - 2, :])
+        for t in range(3):
+            scale_x(1, t, (0, 1))
+        x1_woven = {}
+        for half in range(2):
+            scale_x(1, 3, (half,))
+            x1_woven[half] = kept([P, HALF, PACK], BF16, "x1_woven%d" % half)
+            weave_x(1, half, x1_woven[half][:])
+
+        w3_codes_late = kept([P, PACK - 1, PASS], U32, "w3_codes_late", tag="wgs_then_w3")
+        w3_codes_last = kept([P, PASS], U32, "w3_codes_last")
+        w3_q = {}
+        for n, (a, b) in enumerate([(0, 0), (1, 0), (0, 1), (1, 1)]):
+            codes = w3_codes_late[:, n, :] if n < PACK - 1 else w3_codes_last[:]
+            w3_q[a, b] = quantise_weight(woven3[a, b], codes, "w3_%d%d" % (a, b))
+
+        for half in range(2):
+            codes, scales = quantise_x(x1_woven[half][:].rearrange("p j t -> p (j t)"), HALF, "x1%d" % half)
+            x_q[1, half] = codes[:], scales[:]
+            second_pass(1, half)
+
+        low_q = {}
+
+        lows = {}
+
+        def minimum(half):
+            low = kept([P, 2, HALF, PACK], BF16, "low%d" % half)
+            lows[half] = low
+            for jj in range(2):
+                cols = slice(jj * QUART, (jj + 1) * QUART)
+                for b in range(2):
+                    nc.vector.tensor_tensor(
+                        low[:, b, cols, :].rearrange("p (c i) t -> p c t i", i=4),
+                        y_bank[half, jj, b][:].rearrange("p t (c i) -> p c t i", i=4),
+                        x[b, half][:, :, cols].rearrange("p t (c i) -> p c t i", i=4), MIN)
+
+        def quantise_low(half):
+            low = lows[half]
+            codes = kept([P, 2 * HALF], U32, "low_codes%d" % half)
+            scales = kept([P, 2 * HALF], U8, "low_scales%d" % half)
+            quantise(low[:].rearrange("p b j t -> p (b j t)"), codes[:], scales[:])
+            low_q[half] = codes, scales
+
+        def neighbours(half, b, t):
+            cols = HALF // 16
+            nc.vector.tensor_copy(out=x[b, half][:, t, :],
+                                  in_=page[b, t][:].indirect(idx4[:, half * cols:(half + 1) * cols]))
+            nc.scalar.activation(out=x[b, half][:, t, :], in_=x[b, half][:, t, :], func=ABS,
+                                 scale=near_sb[:, b, t:t + 1])
+
+        q_bank = {}
+
+        def third_product(half):
+            low_codes, low_scales = low_q[half]
+            for b in range(2):
+                for pair in range(2):
+                    q_bank[half, b, pair] = bank(4 * half + 2 * b + pair, [P, 2, HALF], "q_bank%d%d%d" % (half, b, pair))
+                    for tt in range(2):
+                        t = 2 * pair + tt
+                        for a in range(2):
+                            codes, scales = w3_q[a, b]
+                            nc.tensor.matmul_mx(
+                                out=q_bank[half, b, pair][:, tt, :], lhsT=codes[:, t * P:(t + 1) * P].bitcast(FP8X4),
+                                lhsT_scale=scales[:, t * P:(t + 1) * P],
+                                rhs=low_codes[:, a * HALF:(a + 1) * HALF].bitcast(FP8X4),
+                                rhs_scale=low_scales[:, a * HALF:(a + 1) * HALF],
+                                start=(a == 0), stop=(a == 1))
+
+        out_rows = out.rearrange("(b p t) j -> b p t j", b=2, t=PACK)
+
+        def finish(half, b, pair):
+            result = ring.tile([P, 2, HALF], F32, name="result", align_bytes=64)
+            nc.vector.tensor_tensor(result[:], q_bank[half, b, pair][:], x[b, half][:, 2 * pair:2 * pair + 2, :], MULT)
+            nc.sync.dma_start(out_rows[b][:, 2 * pair:2 * pair + 2, half * HALF:(half + 1) * HALF], result[:])
+
+        minimum(0)
+        neighbours(0, 0, 0)
+        quantise_low(0)
+        third_product(0)
+        for b in range(2):
+            for t in range(PACK):
+                if b or t:
+                    neighbours(0, b, t)
+        minimum(1)
+        pairs = [(b, pair) for b in range(2) for pair in range(2)]
+        finish(0, *pairs[0])
+        quantise_low(1)
+        third_product(1)
+        for b, pair in pairs[1:]:
+            finish(0, b, pair)
+        for n, (b, pair) in enumerate(pairs):
+            neighbours(1, b, 2 * pair)
+            neighbours(1, b, 2 * pair + 1)
+            if n > 0:
+                finish(1, *pairs[n - 1])
+        finish(1, *pairs[-1])

@@ -82,27 +82,25 @@ def tile_list_sushi_belt_scores_kernel(
             return tile
 
         tab_sc = kept([P, T], U8, "tab_sc")
-        nc.vector.memset(tab_sc[:].bitcast(I32), 0)
+        nc.gpsimd.memset(tab_sc[:].bitcast(I32), 0)
         for q in range(4):
-            nc.scalar.dma_start(tab_sc[32 * q:32 * q + 12, :].bitcast(I32),
+            nc.gpsimd.dma_start(tab_sc[32 * q:32 * q + 12, :].bitcast(I32),
                                 tab_scales[:, 4 * q:4 * q + 4, :].bitcast(I32))
         w4_sc_raw = kept([P, 2 * H], U8, "w4_sc_raw")
-        nc.vector.memset(w4_sc_raw[:].bitcast(I32), 0)
+        nc.gpsimd.memset(w4_sc_raw[:].bitcast(I32), 0)
         for q in range(4):
-            nc.scalar.dma_start(w4_sc_raw[32 * q:32 * q + 4, :].bitcast(I32).rearrange("r (a c) -> r a c", a=2),
+            nc.gpsimd.dma_start(w4_sc_raw[32 * q:32 * q + 4, :].bitcast(I32).rearrange("r (a c) -> r a c", a=2),
                                 w4_scales[:, 4 * q:4 * q + 4, :].rearrange("a r c -> r a c").bitcast(I32))
 
-        w4_raw = kept([P, 4 * H], U8, "w4_raw")
-        nc.sync.dma_start(w4_raw[:].bitcast(I32).rearrange("p (a c) -> p a c", a=2),
-                          w4_words.rearrange("a p c -> p a c").bitcast(I32))
         raw1 = {}
         raw1[0, 0] = load_weight(w1, 0, 0)
         idx = load_list(offs, "idx")
         raw1[1, 0] = load_weight(w1, 1, 0)
-        tab = [load_table(0)]
         raw1[2, 0] = load_weight(w1, 2, 0)
-        tab.append(load_table(1))
-        tab.append(load_table(2))
+        w4_raw = kept([P, 4 * H], U8, "w4_raw")
+        nc.sync.dma_start(w4_raw[:].bitcast(I32).rearrange("p (a c) -> p a c", a=2),
+                          w4_words.rearrange("a p c -> p a c").bitcast(I32))
+        tab = [load_table(a) for a in range(3)]
         gain_sb = load_rows(gain, "gain_sb")
         idx2 = load_list(offs2, "idx2")
         page = {}
@@ -118,17 +116,6 @@ def tile_list_sushi_belt_scores_kernel(
         raw1[0, 1] = load_weight(w1, 0, 1)
         page[0, 2] = load_page(0, 2)
 
-        w4_codes = kept([P, 4 * H], U8, "w4_codes")
-        w4_sc = kept([P, 2 * H], U8, "w4_sc")
-        for a in range(2):
-            nc.vector.tensor_copy(
-                out=w4_codes[:, a * 2 * H:(a + 1) * 2 * H].bitcast(U16).rearrange("p (b t m) -> p b t m", b=2, t=PACK),
-                in_=w4_raw[:, a * 2 * H:(a + 1) * 2 * H].bitcast(U16).rearrange("p (b m t) -> p b t m", b=2, t=PACK))
-        for a in range(2):
-            nc.vector.tensor_copy(
-                out=w4_sc[:, a * H:(a + 1) * H].rearrange("p (b t m) -> p b t m", b=2, t=PACK),
-                in_=w4_sc_raw[:, a * H:(a + 1) * H].rearrange("p (b m t) -> p b t m", b=2, t=PACK))
-
         v_sc = kept([P, S], U8, "v_sc")
         nc.vector.tensor_copy(out=v_sc[:], in_=tab_sc[:].indirect(idx[:]))
         v = []
@@ -140,36 +127,63 @@ def tile_list_sushi_belt_scores_kernel(
 
         def first_pass(a, b, banks):
             codes, scales = w1_q[a, b]
-            for t in range(PACK):
+            for t, cols, acc in banks:
                 nc.tensor.matmul_mx(
-                    out=banks[t][:], lhsT=codes[:, t * P:(t + 1) * P].bitcast(FP8X4),
-                    lhsT_scale=scales[:, t * P:(t + 1) * P], rhs=v[a][:].bitcast(FP8X4),
-                    rhs_scale=v_sc[4 * a:P, :], start=(a == 0), stop=(a == 2))
+                    out=acc[:], lhsT=codes[:, t * P:(t + 1) * P].bitcast(FP8X4),
+                    lhsT_scale=scales[:, t * P:(t + 1) * P], rhs=v[a][:, cols].bitcast(FP8X4),
+                    rhs_scale=v_sc[4 * a:P, cols], start=(a == 0), stop=(a == 2))
 
-        h = {}
+        h = {(b, t): kept([P, S], F32, "h%d%d" % (b, t)) for b in range(2) for t in range(PACK)}
 
         def leave_h(b, banks):
-            for t in range(PACK):
-                h[b, t] = kept([P, S], F32, "h%d%d" % (b, t))
-                nc.scalar.activation(out=h[b, t][:], in_=banks[t][:], func=COPY, scale=gain_sb[:, b, t:t + 1])
+            for t, cols, acc in banks:
+                nc.scalar.activation(out=h[b, t][:, cols], in_=acc[:], func=COPY, scale=gain_sb[:, b, t:t + 1])
 
-        banks = [bank(t, [P, S], "h_bank0%d" % t) for t in range(PACK)]
-        for a in range(3):
+        halves = [slice(0, HALF), slice(HALF, NJ)]
+        whole = slice(0, NJ)
+
+        def entries(offsets, cols):
+            return offsets[:, cols.start // 16:cols.stop // 16]
+
+        banks = [(0, cols, bank(4 * n, [P, HALF], "h_bank00%d" % n)) for n, cols in enumerate(halves)]
+        banks = banks + [(t, whole, bank(t, [P, S], "h_bank0%d" % t)) for t in range(1, PACK)]
+        for a in range(2):
             prepare_w1(a, 0)
+        w4_codes = kept([P, 4 * H], U8, "w4_codes")
+        w4_sc = kept([P, 2 * H], U8, "w4_sc")
+        for a in range(2):
+            nc.vector.tensor_copy(
+                out=w4_codes[:, a * 2 * H:(a + 1) * 2 * H].bitcast(U16).rearrange("p (b t m) -> p b t m", b=2, t=PACK),
+                in_=w4_raw[:, a * 2 * H:(a + 1) * 2 * H].bitcast(U16).rearrange("p (b m t) -> p b t m", b=2, t=PACK))
+        for a in range(2):
+            nc.vector.tensor_copy(
+                out=w4_sc[:, a * H:(a + 1) * H].rearrange("p (b t m) -> p b t m", b=2, t=PACK),
+                in_=w4_sc_raw[:, a * H:(a + 1) * H].rearrange("p (b m t) -> p b t m", b=2, t=PACK))
+
+        for a in range(3):
             v.append(kept([P, S], U32, "v%d" % a))
-            nc.vector.tensor_copy(out=v[a][:], in_=tab[a][:].bitcast(U32).indirect(idx[:]))
-            first_pass(a, 0, banks)
+            for cols in (halves if a == 2 else [whole]):
+                nc.vector.tensor_copy(out=v[a][:, cols], in_=tab[a][:].bitcast(U32).indirect(entries(idx, cols)))
+            if a == 0:
+                prepare_w1(2, 0)
+        for a in range(3):
+            first_pass(a, 0, banks[:2])
+        for a in range(3):
+            first_pass(a, 0, banks[2:])
         leave_h(0, banks)
 
         reread = {}
 
         def put(b, t):
             weights = wgs_first[:] if t == 0 else wgs_rest[:, t - 1, :]
-            nc.vector.tensor_tensor(page[b, t][:].indirect(idx2[:]), h[b, t][:], weights, MULT)
+            for cols in (halves if (b, t) == (0, 0) else [whole]):
+                nc.vector.tensor_tensor(page[b, t][:].indirect(entries(idx2, cols)), h[b, t][:, cols],
+                                        weights[:, cols], MULT)
 
         def fetch(b, t, into):
             reread[b, t] = into
-            nc.vector.tensor_copy(out=into, in_=page[b, t][:].indirect(idx3[:]))
+            for cols in (halves if (b, t) == (1, PACK - 1) else [whole]):
+                nc.vector.tensor_copy(out=into[:, cols], in_=page[b, t][:].indirect(entries(idx3, cols)))
 
         def fresh_buffer():
             tile = ring.tile([P, NJ], F32, name="reread", align_bytes=64)
@@ -194,7 +208,7 @@ def tile_list_sushi_belt_scores_kernel(
             quantise(woven_flat, codes[:], scales[:])
             return codes, scales
 
-        banks = [bank(PACK + t, [P, S], "h_bank1%d" % t) for t in range(PACK)]
+        banks = [(t, whole, bank(PACK + t, [P, S], "h_bank1%d" % t)) for t in range(PACK)]
         raw1[1, 1] = load_weight(w1, 1, 1)
         page[0, 3] = load_page(0, 3)
         for t in range(3):
@@ -205,20 +219,21 @@ def tile_list_sushi_belt_scores_kernel(
         put(0, 3)
         prepare_w1(1, 1)
         first_pass(1, 1, banks)
-        raw3 = {}
-        raw3[0, 0] = load_weight(w3, 0, 0)
-        page[1, 0] = load_page(1, 0)
+        for t in range(3):
+            page[1, t] = load_page(1, t)
         idx3 = load_list(offs3, "idx3")
         fresh_sb = load_rows(fresh, "fresh_sb")
-        for t in range(1, PACK):
-            page[1, t] = load_page(1, t)
+        page[1, 3] = load_page(1, 3)
         prepare_w1(2, 1)
         first_pass(2, 1, banks)
+        raw3 = {}
+        raw3[0, 0] = load_weight(w3, 0, 0)
         raw3[1, 0] = load_weight(w3, 1, 0)
-        woven3 = {}
-        leave_h(1, banks)
-        woven3[0, 0] = weave_weight(raw3[0, 0])
         raw3[0, 1] = load_weight(w3, 0, 1)
+        raw3[1, 1] = load_weight(w3, 1, 1)
+        idx4 = load_list(offs4, "idx4")
+        near_sb = load_rows(near, "near_sb")
+        leave_h(1, banks)
         for t in range(PACK):
             fetch(0, t, fresh_buffer())
         for t in range(PACK):
@@ -226,12 +241,7 @@ def tile_list_sushi_belt_scores_kernel(
         x0_woven = kept([P, 2, HALF, PACK], BF16, "x0_woven", tag="x0_woven_then_reread")
         for half in range(2):
             weave_x(0, half, x0_woven[:, half, :, :])
-        woven3[1, 0] = weave_weight(raw3[1, 0])
-        raw3[1, 1] = load_weight(w3, 1, 1)
-        idx4 = load_list(offs4, "idx4")
-        near_sb = load_rows(near, "near_sb")
-        woven3[0, 1] = weave_weight(raw3[0, 1])
-        woven3[1, 1] = weave_weight(raw3[1, 1])
+        woven3 = {ab: weave_weight(raw3[ab]) for ab in [(0, 0), (1, 0), (0, 1), (1, 1)]}
         for t in range(PACK):
             put(1, t)
         for t in range(2):
@@ -331,10 +341,11 @@ def tile_list_sushi_belt_scores_kernel(
 
         out_rows = out.rearrange("(b p t) j -> b p t j", b=2, t=PACK)
 
-        def finish(half, b, pair):
-            result = ring.tile([P, 2, HALF], F32, name="result", align_bytes=64)
-            nc.vector.tensor_tensor(result[:], q_bank[half, b, pair][:], x[b, half][:, 2 * pair:2 * pair + 2, :], MULT)
-            nc.sync.dma_start(out_rows[b][:, 2 * pair:2 * pair + 2, half * HALF:(half + 1) * HALF], result[:])
+        def finish(half, b, pair, first=0, count=2):
+            slots = slice(2 * pair + first, 2 * pair + first + count)
+            result = ring.tile([P, count, HALF], F32, name="result", align_bytes=64)
+            nc.vector.tensor_tensor(result[:], q_bank[half, b, pair][:, first:first + count, :], x[b, half][:, slots, :], MULT)
+            nc.sync.dma_start(out_rows[b][:, slots, halves[half]], result[:])
 
         minimum(0)
         neighbours(0, 0, 0)
@@ -356,4 +367,5 @@ def tile_list_sushi_belt_scores_kernel(
             neighbours(1, b, 2 * pair + 1)
             if n > 0:
                 finish(1, *pairs[n - 1])
-        finish(1, *pairs[-1])
+        for first in range(2):
+            finish(1, *pairs[-1], first, 1)

@@ -33,6 +33,7 @@ def tile_list_sushi_belt_scores_kernel(
     with ExitStack() as ctx:
         keep = ctx.enter_context(tc.tile_pool(name="keep", bufs=1))
         ring = ctx.enter_context(tc.tile_pool(name="ring", bufs=4))
+        late = ctx.enter_context(tc.tile_pool(name="late", bufs=1))
         psum = ctx.enter_context(tc.psum_pool(name="psum", bufs=1))
 
         def kept(shape, dtype, name, tag=None):
@@ -51,8 +52,9 @@ def tile_list_sushi_belt_scores_kernel(
             nc.sync.dma_start(tile[:], src.rearrange("(b p t) -> p b t", b=2, t=PACK))
             return tile
 
-        def load_weight(w, a, b):
-            raw = ring.tile([P, PACK, PASS], F32, name="raw", align_bytes=64)
+        def load_weight(w, a, b, raw=None):
+            if raw is None:
+                raw = ring.tile([P, PACK, PASS], F32, name="raw", align_bytes=64)
             nc.sync.dma_start(
                 raw[:], w[a * PASS:(a + 1) * PASS, b * PASS:(b + 1) * PASS].rearrange("(p i) c -> p i c", i=PACK))
             return raw
@@ -81,26 +83,27 @@ def tile_list_sushi_belt_scores_kernel(
             nc.sync.dma_start(tile[:], page0.rearrange("(b p t) c -> b t p c", b=2, t=PACK)[b][t])
             return tile
 
-        tab_sc = kept([P, T], U8, "tab_sc")
-        nc.gpsimd.memset(tab_sc[:].bitcast(I32), 0)
-        for q in range(4):
-            nc.gpsimd.dma_start(tab_sc[32 * q:32 * q + 12, :].bitcast(I32),
-                                tab_scales[:, 4 * q:4 * q + 4, :].bitcast(I32))
-        w4_sc_raw = kept([P, 2 * H], U8, "w4_sc_raw")
-        nc.gpsimd.memset(w4_sc_raw[:].bitcast(I32), 0)
-        for q in range(4):
-            nc.gpsimd.dma_start(w4_sc_raw[32 * q:32 * q + 4, :].bitcast(I32).rearrange("r (a c) -> r a c", a=2),
-                                w4_scales[:, 4 * q:4 * q + 4, :].rearrange("a r c -> r a c").bitcast(I32))
-
         raw1 = {}
         raw1[0, 0] = load_weight(w1, 0, 0)
-        idx = load_list(offs, "idx")
         raw1[1, 0] = load_weight(w1, 1, 0)
+        idx = load_list(offs, "idx")
         raw1[2, 0] = load_weight(w1, 2, 0)
+        tab_sc = kept([P, T], U8, "tab_sc")
+        nc.vector.memset(tab_sc[:].bitcast(I32), 0)
+        for q in range(4):
+            nc.sync.dma_start(tab_sc[32 * q:32 * q + 12, :].bitcast(I32),
+                                tab_scales[:, 4 * q:4 * q + 4, :].bitcast(I32))
         w4_raw = kept([P, 4 * H], U8, "w4_raw")
         nc.sync.dma_start(w4_raw[:].bitcast(I32).rearrange("p (a c) -> p a c", a=2),
                           w4_words.rearrange("a p c -> p a c").bitcast(I32))
-        tab = [load_table(a) for a in range(3)]
+        tab = [load_table(0)]
+        w4_sc_raw = kept([P, 2 * H], U8, "w4_sc_raw")
+        nc.vector.memset(w4_sc_raw[:].bitcast(I32), 0)
+        for q in range(4):
+            nc.sync.dma_start(w4_sc_raw[32 * q:32 * q + 4, :].bitcast(I32).rearrange("r (a c) -> r a c", a=2),
+                                w4_scales[:, 4 * q:4 * q + 4, :].rearrange("a r c -> r a c").bitcast(I32))
+
+        tab = tab + [load_table(1), load_table(2)]
         gain_sb = load_rows(gain, "gain_sb")
         idx2 = load_list(offs2, "idx2")
         page = {}
@@ -117,7 +120,6 @@ def tile_list_sushi_belt_scores_kernel(
         page[0, 2] = load_page(0, 2)
 
         v_sc = kept([P, S], U8, "v_sc")
-        nc.vector.tensor_copy(out=v_sc[:], in_=tab_sc[:].indirect(idx[:]))
         v = []
         w1_q = {}
 
@@ -147,18 +149,15 @@ def tile_list_sushi_belt_scores_kernel(
 
         banks = [(0, cols, bank(4 * n, [P, HALF], "h_bank00%d" % n)) for n, cols in enumerate(halves)]
         banks = banks + [(t, whole, bank(t, [P, S], "h_bank0%d" % t)) for t in range(1, PACK)]
-        for a in range(2):
-            prepare_w1(a, 0)
+        prepare_w1(0, 0)
+        nc.vector.tensor_copy(out=v_sc[:], in_=tab_sc[:].indirect(idx[:]))
+        prepare_w1(1, 0)
         w4_codes = kept([P, 4 * H], U8, "w4_codes")
         w4_sc = kept([P, 2 * H], U8, "w4_sc")
         for a in range(2):
             nc.vector.tensor_copy(
                 out=w4_codes[:, a * 2 * H:(a + 1) * 2 * H].bitcast(U16).rearrange("p (b t m) -> p b t m", b=2, t=PACK),
                 in_=w4_raw[:, a * 2 * H:(a + 1) * 2 * H].bitcast(U16).rearrange("p (b m t) -> p b t m", b=2, t=PACK))
-        for a in range(2):
-            nc.vector.tensor_copy(
-                out=w4_sc[:, a * H:(a + 1) * H].rearrange("p (b t m) -> p b t m", b=2, t=PACK),
-                in_=w4_sc_raw[:, a * H:(a + 1) * H].rearrange("p (b m t) -> p b t m", b=2, t=PACK))
 
         for a in range(3):
             v.append(kept([P, S], U32, "v%d" % a))
@@ -166,6 +165,10 @@ def tile_list_sushi_belt_scores_kernel(
                 nc.vector.tensor_copy(out=v[a][:, cols], in_=tab[a][:].bitcast(U32).indirect(entries(idx, cols)))
             if a == 0:
                 prepare_w1(2, 0)
+                for g in range(2):
+                    nc.vector.tensor_copy(
+                        out=w4_sc[:, g * H:(g + 1) * H].rearrange("p (b t m) -> p b t m", b=2, t=PACK),
+                        in_=w4_sc_raw[:, g * H:(g + 1) * H].rearrange("p (b m t) -> p b t m", b=2, t=PACK))
         for a in range(3):
             first_pass(a, 0, banks[:2])
         for a in range(3):
@@ -189,7 +192,7 @@ def tile_list_sushi_belt_scores_kernel(
             tile = ring.tile([P, NJ], F32, name="reread", align_bytes=64)
             return tile[:]
 
-        x = {(b, half): kept([P, PACK, HALF], F32, "x%d%d" % (b, half)) for b in range(2) for half in range(2)}
+        x = {(0, half): kept([P, PACK, HALF], F32, "x0%d" % half) for half in range(2)}
 
         def scale_x(b, t, halves):
             for half in halves:
@@ -219,21 +222,23 @@ def tile_list_sushi_belt_scores_kernel(
         put(0, 3)
         prepare_w1(1, 1)
         first_pass(1, 1, banks)
-        for t in range(3):
-            page[1, t] = load_page(1, t)
-        idx3 = load_list(offs3, "idx3")
-        fresh_sb = load_rows(fresh, "fresh_sb")
-        page[1, 3] = load_page(1, 3)
-        prepare_w1(2, 1)
-        first_pass(2, 1, banks)
         raw3 = {}
         raw3[0, 0] = load_weight(w3, 0, 0)
+        page[1, 0] = load_page(1, 0)
+        idx3 = load_list(offs3, "idx3")
+        fresh_sb = load_rows(fresh, "fresh_sb")
+        for t in range(1, PACK):
+            page[1, t] = load_page(1, t)
+        prepare_w1(2, 1)
+        first_pass(2, 1, banks)
         raw3[1, 0] = load_weight(w3, 1, 0)
         raw3[0, 1] = load_weight(w3, 0, 1)
-        raw3[1, 1] = load_weight(w3, 1, 1)
+        raw_last = late.tile([P, PACK, PASS], F32, name="raw_last", align_bytes=64, offset=0)
+        raw3[1, 1] = load_weight(w3, 1, 1, raw_last)
         idx4 = load_list(offs4, "idx4")
         near_sb = load_rows(near, "near_sb")
         leave_h(1, banks)
+        woven3 = {(0, 0): weave_weight(raw3[0, 0])}
         for t in range(PACK):
             fetch(0, t, fresh_buffer())
         for t in range(PACK):
@@ -241,11 +246,11 @@ def tile_list_sushi_belt_scores_kernel(
         x0_woven = kept([P, 2, HALF, PACK], BF16, "x0_woven", tag="x0_woven_then_reread")
         for half in range(2):
             weave_x(0, half, x0_woven[:, half, :, :])
-        woven3 = {ab: weave_weight(raw3[ab]) for ab in [(0, 0), (1, 0), (0, 1), (1, 1)]}
+        for ab in [(1, 0), (0, 1), (1, 1)]:
+            woven3[ab] = weave_weight(raw3[ab])
         for t in range(PACK):
             put(1, t)
-        for t in range(2):
-            fetch(1, t, fresh_buffer())
+        fetch(1, 0, fresh_buffer())
         codes, scales = quantise_x(x0_woven[:].rearrange("p h j t -> p (h j t)"), NJ, "x0")
         for half in range(2):
             x_q[0, half] = codes[:, half * HALF:(half + 1) * HALF], scales[:, half * HALF:(half + 1) * HALF]
@@ -269,9 +274,11 @@ def tile_list_sushi_belt_scores_kernel(
 
         for half in range(2):
             second_pass(0, half)
-        reread_late = kept([P, 2, NJ], F32, "reread_late", tag="x0_woven_then_reread")
-        for t in range(2, PACK):
-            fetch(1, t, reread_late[:, t - 2, :])
+        reread_late = kept([P, PACK - 1, NJ], F32, "reread_late", tag="x0_woven_then_reread")
+        for t in range(1, PACK):
+            fetch(1, t, reread_late[:, t - 1, :])
+        for half in range(2):
+            x[1, half] = late.tile([P, PACK, HALF], F32, name="x1%d" % half, align_bytes=64, offset=half * PACK * HALF * 4)
         for t in range(3):
             scale_x(1, t, (0, 1))
         x1_woven = {}

@@ -61,8 +61,8 @@ def tile_list_sushi_belt_scores_kernel(
 
         def weave_weight(raw):
             woven = ring.tile([P, PACK, P, PACK], BF16, name="woven", align_bytes=64)
-            nc.scalar.copy(out=woven[:].rearrange("p t m i -> p m i t"),
-                           in_=raw[:].rearrange("p i (m t) -> p m i t", t=PACK))
+            nc.scalar.copy(out=woven[:].rearrange("p t m i -> p m t i"),
+                           in_=raw[:].rearrange("p i (m t) -> p m t i", t=PACK))
             return woven
 
         def quantise(woven_flat, codes, scales):
@@ -200,8 +200,8 @@ def tile_list_sushi_belt_scores_kernel(
                                      func=COPY, scale=fresh_sb[:, b, t:t + 1])
 
         def weave_x(b, half, woven):
-            nc.scalar.copy(out=woven.rearrange("p (c i) t -> p c t i", i=4),
-                           in_=x[b, half][:].rearrange("p t (c i) -> p c t i", i=4))
+            nc.scalar.copy(out=woven.rearrange("p (c i) t -> p c t i", i=2),
+                           in_=x[b, half][:].rearrange("p t (c i) -> p c t i", i=2))
 
         x_q = {}
 
@@ -310,9 +310,9 @@ def tile_list_sushi_belt_scores_kernel(
                 cols = slice(jj * QUART, (jj + 1) * QUART)
                 for b in range(2):
                     nc.vector.tensor_tensor(
-                        low[:, b, cols, :].rearrange("p (c i) t -> p c t i", i=4),
-                        y_bank[half, jj, b][:].rearrange("p t (c i) -> p c t i", i=4),
-                        x[b, half][:, :, cols].rearrange("p t (c i) -> p c t i", i=4), MIN)
+                        low[:, b, cols, :].rearrange("p (c i) t -> p c t i", i=2),
+                        y_bank[half, jj, b][:].rearrange("p t (c i) -> p c t i", i=2),
+                        x[b, half][:, :, cols].rearrange("p t (c i) -> p c t i", i=2), MIN)
 
         def quantise_low(half):
             low = lows[half]

@@ -83,26 +83,25 @@ def tile_list_sushi_belt_scores_kernel(
             nc.sync.dma_start(tile[:], page0.rearrange("(b p t) c -> b t p c", b=2, t=PACK)[b][t])
             return tile
 
+        w4_raw = kept([P, 4 * H], U8, "w4_raw")
+        nc.sync.dma_start(w4_raw[:].bitcast(I32).rearrange("p (a c) -> p a c", a=2),
+                          w4_words.rearrange("a p c -> p a c").bitcast(I32))
         raw1 = {}
         raw1[0, 0] = load_weight(w1, 0, 0)
-        raw1[1, 0] = load_weight(w1, 1, 0)
         idx = load_list(offs, "idx")
+        raw1[1, 0] = load_weight(w1, 1, 0)
         raw1[2, 0] = load_weight(w1, 2, 0)
         tab_sc = kept([P, T], U8, "tab_sc")
         nc.vector.memset(tab_sc[:].bitcast(I32), 0)
         for q in range(4):
             nc.sync.dma_start(tab_sc[32 * q:32 * q + 12, :].bitcast(I32),
-                                tab_scales[:, 4 * q:4 * q + 4, :].bitcast(I32))
-        w4_raw = kept([P, 4 * H], U8, "w4_raw")
-        nc.sync.dma_start(w4_raw[:].bitcast(I32).rearrange("p (a c) -> p a c", a=2),
-                          w4_words.rearrange("a p c -> p a c").bitcast(I32))
+                              tab_scales[:, 4 * q:4 * q + 4, :].bitcast(I32))
         tab = [load_table(0)]
         w4_sc_raw = kept([P, 2 * H], U8, "w4_sc_raw")
         nc.vector.memset(w4_sc_raw[:].bitcast(I32), 0)
         for q in range(4):
             nc.sync.dma_start(w4_sc_raw[32 * q:32 * q + 4, :].bitcast(I32).rearrange("r (a c) -> r a c", a=2),
-                                w4_scales[:, 4 * q:4 * q + 4, :].rearrange("a r c -> r a c").bitcast(I32))
-
+                              w4_scales[:, 4 * q:4 * q + 4, :].rearrange("a r c -> r a c").bitcast(I32))
         tab = tab + [load_table(1), load_table(2)]
         gain_sb = load_rows(gain, "gain_sb")
         idx2 = load_list(offs2, "idx2")
@@ -149,16 +148,15 @@ def tile_list_sushi_belt_scores_kernel(
 
         banks = [(0, cols, bank(4 * n, [P, HALF], "h_bank00%d" % n)) for n, cols in enumerate(halves)]
         banks = banks + [(t, whole, bank(t, [P, S], "h_bank0%d" % t)) for t in range(1, PACK)]
-        prepare_w1(0, 0)
-        nc.vector.tensor_copy(out=v_sc[:], in_=tab_sc[:].indirect(idx[:]))
-        prepare_w1(1, 0)
         w4_codes = kept([P, 4 * H], U8, "w4_codes")
         w4_sc = kept([P, 2 * H], U8, "w4_sc")
         for a in range(2):
             nc.vector.tensor_copy(
                 out=w4_codes[:, a * 2 * H:(a + 1) * 2 * H].bitcast(U16).rearrange("p (b t m) -> p b t m", b=2, t=PACK),
                 in_=w4_raw[:, a * 2 * H:(a + 1) * 2 * H].bitcast(U16).rearrange("p (b m t) -> p b t m", b=2, t=PACK))
-
+        prepare_w1(0, 0)
+        prepare_w1(1, 0)
+        nc.vector.tensor_copy(out=v_sc[:], in_=tab_sc[:].indirect(idx[:]))
         for a in range(3):
             v.append(kept([P, S], U32, "v%d" % a))
             for cols in (halves if a == 2 else [whole]):
@@ -348,6 +346,13 @@ def tile_list_sushi_belt_scores_kernel(
 
         out_rows = out.rearrange("(b p t) j -> b p t j", b=2, t=PACK)
 
+        def finish_aside(half, b, pair):
+            slots = slice(2 * pair, 2 * pair + 2)
+            product = ring.tile([P, 2, HALF], F32, name="product", align_bytes=64)
+            nc.scalar.copy(out=product[:], in_=q_bank[half, b, pair][:])
+            nc.gpsimd.tensor_tensor(product[:], product[:], x[b, half][:, slots, :], MULT)
+            nc.sync.dma_start(out_rows[b][:, slots, halves[half]], product[:])
+
         def finish(half, b, pair, first=0, count=2):
             slots = slice(2 * pair + first, 2 * pair + first + count)
             result = ring.tile([P, count, HALF], F32, name="result", align_bytes=64)
@@ -362,17 +367,17 @@ def tile_list_sushi_belt_scores_kernel(
             for t in range(PACK):
                 if b or t:
                     neighbours(0, b, t)
-        minimum(1)
         pairs = [(b, pair) for b in range(2) for pair in range(2)]
-        finish(0, *pairs[0])
+        for b, pair in pairs:
+            finish_aside(0, b, pair)
+        minimum(1)
+        neighbours(1, 0, 0)
         quantise_low(1)
         third_product(1)
-        for b, pair in pairs[1:]:
-            finish(0, b, pair)
-        for n, (b, pair) in enumerate(pairs):
+        neighbours(1, 0, 1)
+        for n, (b, pair) in enumerate(pairs[1:]):
             neighbours(1, b, 2 * pair)
             neighbours(1, b, 2 * pair + 1)
-            if n > 0:
-                finish(1, *pairs[n - 1])
+            finish(1, *pairs[n])
         for first in range(2):
             finish(1, *pairs[-1], first, 1)

from contextlib import ExitStack

import concourse.mybir as mybir

K, T, S, H, T2, NJ = 1536, 2048, 512, 1024, 1024, 512
FLOPS = 2 * K * H * S + 2 * 2 * H * H * NJ

F32 = mybir.dt.float32
BF16 = mybir.dt.bfloat16
I32 = mybir.dt.int32
U32 = mybir.dt.uint32
U16 = mybir.dt.uint16
U8 = mybir.dt.uint8
FP8X4 = mybir.dt.float8_e4m3fn_x4
FP4X4 = mybir.dt.float4_e2m1fn_x4
MULT = mybir.AluOpType.mult
MIN = mybir.AluOpType.min
COPY = mybir.ActivationFunctionType.Copy
ABS = mybir.ActivationFunctionType.Abs

P = 128
PACK = 4
PASS = P * PACK
HALF = NJ // 2
QUART = NJ // 4


def tile_list_sushi_belt_scores_kernel(
    tc, tab_words, tab_scales, offs, offs2, offs3, offs4, w1, gain, wgs, page0, fresh,
    w4_words, w4_scales, w3, near, out,
):
    nc = tc.nc
    with ExitStack() as ctx:
        keep = ctx.enter_context(tc.tile_pool(name="keep", bufs=1))
        ring = ctx.enter_context(tc.tile_pool(name="ring", bufs=4))
        late = ctx.enter_context(tc.tile_pool(name="late", bufs=1))
        psum = ctx.enter_context(tc.psum_pool(name="psum", bufs=1))

        def kept(shape, dtype, name, tag=None):
            return keep.tile(shape, dtype, name=name, tag=tag or name, align_bytes=64)

        def bank(index, shape, name):
            return psum.tile(shape, F32, name=name, tag="bank%d" % index)

        def load_list(src, name):
            tile = keep.tile([P, 32], U16, name=name)
            nc.sync.dma_start(tile[:], src)
            return tile

        def load_rows(src, name):
            tile = kept([P, 2, PACK], F32, name)
            nc.sync.dma_start(tile[:], src.rearrange("(b p t) -> p b t", b=2, t=PACK))
            return tile

        def load_weight(w, a, b, raw=None):
            if raw is None:
                raw = ring.tile([P, PACK, PASS], F32, name="raw", align_bytes=64)
            nc.sync.dma_start(
                raw[:], w[a * PASS:(a + 1) * PASS, b * PASS:(b + 1) * PASS].rearrange("(p i) c -> p i c", i=PACK))
            return raw

        def weave_weight(raw):
            woven = ring.tile([P, PACK, P, PACK], BF16, name="woven", align_bytes=64)
            nc.scalar.copy(out=woven[:].rearrange("p t m i -> p m t i"),
                           in_=raw[:].rearrange("p i (m t) -> p m t i", t=PACK))
            return woven

        def quantise(woven_flat, codes, scales):
            nc.vector.quantize_mx(out=codes.bitcast(FP8X4), scales=scales, in_=woven_flat)

        def quantise_weight(woven, codes, name):
            scales = kept([P, PASS], U8, name + "_scales")
            quantise(woven[:].rearrange("p t m i -> p (t m i)"), codes, scales[:])
            return codes, scales

        def load_table(a):
            tile = kept([P, T], I32, "tab%d" % a)
            nc.sync.dma_start(tile[:], tab_words[a].rearrange("p t i -> p (t i)").bitcast(I32))
            return tile

        def load_page(b, t):
            tile = kept([P, T2], F32, "page%d%d" % (b, t))
            nc.sync.dma_start(tile[:], page0.rearrange("(b p t) c -> b t p c", b=2, t=PACK)[b][t])
            return tile

        w4_raw = kept([P, 4 * H], U8, "w4_raw")
        nc.sync.dma_start(w4_raw[:].bitcast(I32).rearrange("p (a c) -> p a c", a=2),
                          w4_words.rearrange("a p c -> p a c").bitcast(I32))
        raw1 = {}
        raw1[0, 0] = load_weight(w1, 0, 0)
        idx = load_list(offs, "idx")
        raw1[1, 0] = load_weight(w1, 1, 0)
        raw1[2, 0] = load_weight(w1, 2, 0)
        tab_sc = kept([P, T], U8, "tab_sc")
        nc.vector.memset(tab_sc[:].bitcast(I32), 0)
        for q in range(4):
            nc.sync.dma_start(tab_sc[32 * q:32 * q + 12, :].bitcast(I32),
                              tab_scales[:, 4 * q:4 * q + 4, :].bitcast(I32))
        tab = [load_table(0)]
        w4_sc_raw = kept([P, 2 * H], U8, "w4_sc_raw")
        nc.vector.memset(w4_sc_raw[:].bitcast(I32), 0)
        for q in range(4):
            nc.sync.dma_start(w4_sc_raw[32 * q:32 * q + 4, :].bitcast(I32).rearrange("r (a c) -> r a c", a=2),
                              w4_scales[:, 4 * q:4 * q + 4, :].rearrange("a r c -> r a c").bitcast(I32))
        tab = tab + [load_table(1), load_table(2)]
        gain_sb = load_rows(gain, "gain_sb")
        idx2 = load_list(offs2, "idx2")
        page = {}
        page[0, 0] = load_page(0, 0)
        wgs_rows = wgs.rearrange("(q t) j -> q t j", t=PACK)
        wgs_first = kept([P, S], F32, "wgs_first")
        for g in range(4):
            nc.sync.dma_start(wgs_first[32 * g:32 * g + 32, :], wgs_rows[:, 0, :])
        page[0, 1] = load_page(0, 1)
        wgs_rest = kept([P, PACK - 1, S], F32, "wgs_rest", tag="wgs_then_w3")
        for g in range(4):
            nc.sync.dma_start(wgs_rest[32 * g:32 * g + 32, :, :], wgs_rows[:, 1:PACK, :])
        raw1[0, 1] = load_weight(w1, 0, 1)
        page[0, 2] = load_page(0, 2)

        v_sc = kept([P, S], U8, "v_sc")
        v = []
        w1_q = {}

        def prepare_w1(a, b):
            codes = kept([P, PASS], U32, "w1_codes%d%d" % (a, b))
            w1_q[a, b] = quantise_weight(weave_weight(raw1[a, b]), codes[:], "w1_%d%d" % (a, b))

        def first_pass(a, b, banks):
            codes, scales = w1_q[a, b]
            for t, cols, acc in banks:
                nc.tensor.matmul_mx(
                    out=acc[:], lhsT=codes[:, t * P:(t + 1) * P].bitcast(FP8X4),
                    lhsT_scale=scales[:, t * P:(t + 1) * P], rhs=v[a][:, cols].bitcast(FP8X4),
                    rhs_scale=v_sc[4 * a:P, cols], start=(a == 0), stop=(a == 2))

        h = {(b, t): kept([P, S], F32, "h%d%d" % (b, t)) for b in range(2) for t in range(PACK)}

        def leave_h(b, banks):
            for t, cols, acc in banks:
                nc.scalar.activation(out=h[b, t][:, cols], in_=acc[:], func=COPY, scale=gain_sb[:, b, t:t + 1])

        halves = [slice(0, HALF), slice(HALF, NJ)]
        whole = slice(0, NJ)

        def entries(offsets, cols):
            return offsets[:, cols.start // 16:cols.stop // 16]

        banks = [(0, cols, bank(4 * n, [P, HALF], "h_bank00%d" % n)) for n, cols in enumerate(halves)]
        banks = banks + [(t, whole, bank(t, [P, S], "h_bank0%d" % t)) for t in range(1, PACK)]
        w4_codes = kept([P, 4 * H], U8, "w4_codes")
        w4_sc = kept([P, 2 * H], U8, "w4_sc")
        for a in range(2):
            nc.vector.tensor_copy(
                out=w4_codes[:, a * 2 * H:(a + 1) * 2 * H].bitcast(U16).rearrange("p (b t m) -> p b t m", b=2, t=PACK),
                in_=w4_raw[:, a * 2 * H:(a + 1) * 2 * H].bitcast(U16).rearrange("p (b m t) -> p b t m", b=2, t=PACK))
        prepare_w1(0, 0)
        prepare_w1(1, 0)
        nc.vector.tensor_copy(out=v_sc[:], in_=tab_sc[:].indirect(idx[:]))
        for a in range(3):
            v.append(kept([P, S], U32, "v%d" % a))
            for cols in (halves if a == 2 else [whole]):
                nc.vector.tensor_copy(out=v[a][:, cols], in_=tab[a][:].bitcast(U32).indirect(entries(idx, cols)))
            if a == 0:
                prepare_w1(2, 0)
                for g in range(2):
                    nc.vector.tensor_copy(
                        out=w4_sc[:, g * H:(g + 1) * H].rearrange("p (b t m) -> p b t m", b=2, t=PACK),
                        in_=w4_sc_raw[:, g * H:(g + 1) * H].rearrange("p (b m t) -> p b t m", b=2, t=PACK))
        for a in range(3):
            first_pass(a, 0, banks[:2])
        for a in range(3):
            first_pass(a, 0, banks[2:])
        leave_h(0, banks)

        reread = {}

        def put(b, t):
            weights = wgs_first[:] if t == 0 else wgs_rest[:, t - 1, :]
            for cols in (halves if (b, t) == (0, 0) else [whole]):
                nc.vector.tensor_tensor(page[b, t][:].indirect(entries(idx2, cols)), h[b, t][:, cols],
                                        weights[:, cols], MULT)

        def fetch(b, t, into):
            reread[b, t] = into
            for cols in (halves if (b, t) == (1, PACK - 1) else [whole]):
                nc.vector.tensor_copy(out=into[:, cols], in_=page[b, t][:].indirect(entries(idx3, cols)))

        def fresh_buffer():
            tile = ring.tile([P, NJ], F32, name="reread", align_bytes=64)
            return tile[:]

        x = {(0, half): kept([P, PACK, HALF], F32, "x0%d" % half) for half in range(2)}

        def scale_x(b, t, halves):
            for half in halves:
                nc.scalar.activation(out=x[b, half][:, t, :], in_=reread[b, t][:, half * HALF:(half + 1) * HALF],
                                     func=COPY, scale=fresh_sb[:, b, t:t + 1])

        def weave_x(b, half, woven):
            nc.scalar.copy(out=woven.rearrange("p (c i) t -> p c t i", i=2),
                           in_=x[b, half][:].rearrange("p t (c i) -> p c t i", i=2))

        x_q = {}

        def quantise_x(woven_flat, width, name):
            codes = kept([P, width], U32, name + "_codes")
            scales = kept([P, width], U8, name + "_scales")
            quantise(woven_flat, codes[:], scales[:])
            return codes, scales

        banks = [(t, whole, bank(PACK + t, [P, S], "h_bank1%d" % t)) for t in range(PACK)]
        raw1[1, 1] = load_weight(w1, 1, 1)
        page[0, 3] = load_page(0, 3)
        for t in range(3):
            put(0, t)
        prepare_w1(0, 1)
        first_pass(0, 1, banks)
        raw1[2, 1] = load_weight(w1, 2, 1)
        put(0, 3)
        prepare_w1(1, 1)
        first_pass(1, 1, banks)
        raw3 = {}
        raw3[0, 0] = load_weight(w3, 0, 0)
        page[1, 0] = load_page(1, 0)
        idx3 = load_list(offs3, "idx3")
        fresh_sb = load_rows(fresh, "fresh_sb")
        for t in range(1, PACK):
            page[1, t] = load_page(1, t)
        prepare_w1(2, 1)
        first_pass(2, 1, banks)
        raw3[1, 0] = load_weight(w3, 1, 0)
        raw3[0, 1] = load_weight(w3, 0, 1)
        raw_last = late.tile([P, PACK, PASS], F32, name="raw_last", align_bytes=64, offset=0)
        raw3[1, 1] = load_weight(w3, 1, 1, raw_last)
        idx4 = load_list(offs4, "idx4")
        near_sb = load_rows(near, "near_sb")
        leave_h(1, banks)
        woven3 = {(0, 0): weave_weight(raw3[0, 0])}
        for t in range(PACK):
            fetch(0, t, fresh_buffer())
        for t in range(PACK):
            scale_x(0, t, (0, 1))
        x0_woven = kept([P, 2, HALF, PACK], BF16, "x0_woven", tag="x0_woven_then_reread")
        for half in range(2):
            weave_x(0, half, x0_woven[:, half, :, :])
        for ab in [(1, 0), (0, 1), (1, 1)]:
            woven3[ab] = weave_weight(raw3[ab])
        for t in range(PACK):
            put(1, t)
        fetch(1, 0, fresh_buffer())
        codes, scales = quantise_x(x0_woven[:].rearrange("p h j t -> p (h j t)"), NJ, "x0")
        for half in range(2):
            x_q[0, half] = codes[:, half * HALF:(half + 1) * HALF], scales[:, half * HALF:(half + 1) * HALF]

        y_bank = {(half, jj, b): bank(4 * half + 2 * jj + b, [P, PACK, QUART], "y_bank%d%d%d" % (half, jj, b))
                  for half in range(2) for jj in range(2) for b in range(2)}

        def second_pass(a, half):
            codes, scales = x_q[a, half]
            for jj in range(2):
                for b in range(2):
                    for t in range(PACK):
                        col = a * H + b * PASS + t * P
                        nc.tensor.matmul_mx(
                            out=y_bank[half, jj, b][:, t, :],
                            lhsT=w4_codes[:, 2 * col:2 * (col + P)].bitcast(FP4X4),
                            lhsT_scale=w4_sc[:, col:col + P],
                            rhs=codes[:, jj * QUART:(jj + 1) * QUART].bitcast(FP8X4),
                            rhs_scale=scales[:, jj * QUART:(jj + 1) * QUART],
                            start=(a == 0 and t == 0), stop=(a == 1 and t == PACK - 1))

        for half in range(2):
            second_pass(0, half)
        reread_late = kept([P, PACK - 1, NJ], F32, "reread_late", tag="x0_woven_then_reread")
        for t in range(1, PACK):
            fetch(1, t, reread_late[:, t - 1, :])
        for half in range(2):
            x[1, half] = late.tile([P, PACK, HALF], F32, name="x1%d" % half, align_bytes=64, offset=half * PACK * HALF * 4)
        for t in range(3):
            scale_x(1, t, (0, 1))
        x1_woven = {}
        for half in range(2):
            scale_x(1, 3, (half,))
            x1_woven[half] = kept([P, HALF, PACK], BF16, "x1_woven%d" % half)
            weave_x(1, half, x1_woven[half][:])

        w3_codes_late = kept([P, PACK - 1, PASS], U32, "w3_codes_late", tag="wgs_then_w3")
        w3_codes_last = kept([P, PASS], U32, "w3_codes_last")
        w3_q = {}
        for n, (a, b) in enumerate([(0, 0), (1, 0), (0, 1), (1, 1)]):
            codes = w3_codes_late[:, n, :] if n < PACK - 1 else w3_codes_last[:]
            w3_q[a, b] = quantise_weight(woven3[a, b], codes, "w3_%d%d" % (a, b))

        for half in range(2):
            codes, scales = quantise_x(x1_woven[half][:].rearrange("p j t -> p (j t)"), HALF, "x1%d" % half)
            x_q[1, half] = codes[:], scales[:]
            second_pass(1, half)

        low_q = {}

        lows = {}

        def minimum(half):
            low = kept([P, 2, HALF, PACK], BF16, "low%d" % half)
            lows[half] = low
            for jj in range(2):
                cols = slice(jj * QUART, (jj + 1) * QUART)
                for b in range(2):
                    nc.vector.tensor_tensor(
                        low[:, b, cols, :].rearrange("p (c i) t -> p c t i", i=2),
                        y_bank[half, jj, b][:].rearrange("p t (c i) -> p c t i", i=2),
                        x[b, half][:, :, cols].rearrange("p t (c i) -> p c t i", i=2), MIN)

        def quantise_low(half):
            low = lows[half]
            codes = kept([P, 2 * HALF], U32, "low_codes%d" % half)
            scales = kept([P, 2 * HALF], U8, "low_scales%d" % half)
            quantise(low[:].rearrange("p b j t -> p (b j t)"), codes[:], scales[:])
            low_q[half] = codes, scales

        def neighbours(half, b, t):
            cols = HALF // 16
            nc.vector.tensor_copy(out=x[b, half][:, t, :],
                                  in_=page[b, t][:].indirect(idx4[:, half * cols:(half + 1) * cols]))
            nc.scalar.activation(out=x[b, half][:, t, :], in_=x[b, half][:, t, :], func=ABS,
                                 scale=near_sb[:, b, t:t + 1])

        q_bank = {}

        def third_product(half):
            low_codes, low_scales = low_q[half]
            for b in range(2):
                for pair in range(2):
                    q_bank[half, b, pair] = bank(4 * half + 2 * b + pair, [P, 2, HALF], "q_bank%d%d%d" % (half, b, pair))
                    for tt in range(2):
                        t = 2 * pair + tt
                        for a in range(2):
                            codes, scales = w3_q[a, b]
                            nc.tensor.matmul_mx(
                                out=q_bank[half, b, pair][:, tt, :], lhsT=codes[:, t * P:(t + 1) * P].bitcast(FP8X4),
                                lhsT_scale=scales[:, t * P:(t + 1) * P],
                                rhs=low_codes[:, a * HALF:(a + 1) * HALF].bitcast(FP8X4),
                                rhs_scale=low_scales[:, a * HALF:(a + 1) * HALF],
                                start=(a == 0), stop=(a == 1))

        out_rows = out.rearrange("(b p t) j -> b p t j", b=2, t=PACK)

        def finish_aside(half, b, pair):
            slots = slice(2 * pair, 2 * pair + 2)
            product = ring.tile([P, 2, HALF], F32, name="product", align_bytes=64)
            nc.scalar.copy(out=product[:], in_=q_bank[half, b, pair][:])
            nc.gpsimd.tensor_tensor(product[:], product[:], x[b, half][:, slots, :], MULT)
            nc.sync.dma_start(out_rows[b][:, slots, halves[half]], product[:])

        def finish(half, b, pair, first=0, count=2):
            slots = slice(2 * pair + first, 2 * pair + first + count)
            result = ring.tile([P, count, HALF], F32, name="result", align_bytes=64)
            nc.vector.tensor_tensor(result[:], q_bank[half, b, pair][:, first:first + count, :], x[b, half][:, slots, :], MULT)
            nc.sync.dma_start(out_rows[b][:, slots, halves[half]], result[:])

        minimum(0)
        neighbours(0, 0, 0)
        quantise_low(0)
        third_product(0)
        for b in range(2):
            for t in range(PACK):
                if b or t:
                    neighbours(0, b, t)
        pairs = [(b, pair) for b in range(2) for pair in range(2)]
        for b, pair in pairs:
            finish_aside(0, b, pair)
        minimum(1)
        neighbours(1, 0, 0)
        quantise_low(1)
        third_product(1)
        neighbours(1, 0, 1)
        for n, (b, pair) in enumerate(pairs[1:]):
            neighbours(1, b, 2 * pair)
            neighbours(1, b, 2 * pair + 1)
            finish(1, *pairs[n])
        for first in range(2):
            finish(1, *pairs[-1], first, 1)
